import numpy as np
import ml_dtypes


def mxq(x, axis, fmt="e4m3"):
    dtype, down = {"e4m3": (ml_dtypes.float8_e4m3fn, 7), "e5m2": (ml_dtypes.float8_e5m2, 14)}[fmt]
    v = np.moveaxis(np.asarray(x, np.float32).astype(ml_dtypes.bfloat16).astype(np.float64), axis, -1)
    blocks = v.reshape(v.shape[:-1] + (-1, 32))
    amax = np.abs(blocks).max(-1, keepdims=True)
    byte = np.maximum(np.where(amax > 0, np.frexp(amax)[1] - 1 + 127, 0) - down, 1)
    scale = np.exp2(byte - 127.0)
    codes = (blocks / scale).astype(np.float32).astype(dtype).astype(np.float64)
    return np.moveaxis((codes * scale).reshape(v.shape), -1, axis)


WIDE = False


def mx_kscale(k):
    if not WIDE:
        return np.ones(k)
    levels = np.array([10, -10, 5, -5, 0])
    if k % 512:
        return np.exp2(np.random.permutation(np.resize(levels, k // 32))).repeat(32)
    a = np.empty((k // 512, 16))
    for p in range(k // 512):
        a[p, :8] = np.random.permutation(np.resize(levels, 8))
        for g in range(8):
            far = levels[np.abs(levels - a[p, g]) >= 10]
            a[p, g + 8] = far[np.random.randint(len(far))]
    return np.exp2(a.ravel()).repeat(32)


def f64(x):
    return np.asarray(x).astype(np.float64)


def striped(idx):
    return np.tile(idx.reshape(-1, 16).T, (8, 1)).astype(np.uint16)


def unstriped(offs):
    return offs[:16].T.reshape(-1).astype(np.int64)


def relu(v):
    return np.maximum(v, 0.0)


K, T, S, V, N, U = 512, 1024, 512, 256, 256, 512


def setup_inputs():
    n = np.random.standard_normal
    s = mx_kscale(K)[:, None]
    return {
        "xT": (n((K, T)) * s).astype(np.float32),
        "w1": (n((K, N)) / np.sqrt(2 * K) / s).astype(np.float32),
        "w2": (n((K, N)) / np.sqrt(2 * K) / s).astype(np.float32),
        "offs": striped(np.random.permutation(T)[:S]),
        "to1": striped(np.random.permutation(U)[:V]),
        "to2": striped(np.random.permutation(U)[:V]),
    }


def reference(xT, w1, w2, offs, to1, to2):
    xq = mxq(f64(xT)[:, unstriped(offs)], 0, "e4m3")
    o0 = np.zeros((N, S))
    o0[:, unstriped(to1)] = mxq(f64(w1), 0, "e4m3").T @ xq[:, :V]
    o1 = np.zeros((N, S))
    o1[:, unstriped(to2)] = mxq(f64(w2), 0, "e4m3").T @ xq[:, V:2 * V]
    return relu(o0 + o1)

@@ -1,0 +1,129 @@
+from contextlib import ExitStack
+
+import concourse.mybir as mybir
+
+K, T, S, V, N, U = 512, 1024, 512, 256, 256, 512
+FLOPS = 2 * K * N * S
+
+F32 = mybir.dt.float32
+BF16 = mybir.dt.bfloat16
+U32 = mybir.dt.uint32
+U16 = mybir.dt.uint16
+U8 = mybir.dt.uint8
+FP8X4 = mybir.dt.float8_e4m3fn_x4
+ADD = mybir.AluOpType.add
+RELU = mybir.ActivationFunctionType.Relu
+
+P = 128
+PACK = 4
+TAPS = 2
+BLOCKS = N // P
+LIST = 16
+
+
+def tile_picked_spconv_relu_e_kernel(tc, xT, w1, w2, offs, to1, to2, out):
+    nc = tc.nc
+    with ExitStack() as ctx:
+        keep = ctx.enter_context(tc.tile_pool(name="keep", bufs=1))
+        psum = ctx.enter_context(tc.psum_pool(name="psum", bufs=1))
+
+        offs_sb = keep.tile([P, S // LIST], U16, name="offs_sb")
+        to_sb = [keep.tile([P, V // LIST], U16, name="to_sb%d" % d) for d in range(TAPS)]
+        x_rows = xT.rearrange("(p j) t -> p j t", j=PACK)
+        x_sb = [keep.tile([P, T], F32, name="x_sb%d" % j) for j in range(PACK)]
+        w_sb = [keep.tile([P, PACK, N], F32, name="w_sb%d" % d) for d in range(TAPS)]
+
+        nc.sync.dma_start(x_sb[0][:], x_rows[:, 0, :])
+        nc.sync.dma_start(offs_sb[:], offs)
+        for j in range(1, PACK):
+            nc.sync.dma_start(x_sb[j][:], x_rows[:, j, :])
+        for d, (w, to) in enumerate(((w1, to1), (w2, to2))):
+            nc.sync.dma_start(w_sb[d][:], w.rearrange("(p j) n -> p j n", j=PACK))
+            nc.sync.dma_start(to_sb[d][:], to)
+
+        cells = [[keep.tile([P, U], F32, name="cells%d_%d" % (d, b)) for b in range(BLOCKS)] for d in range(TAPS)]
+        for d in range(TAPS):
+            for b in range(BLOCKS):
+                (nc.vector if d == 0 else nc.gpsimd).memset(cells[d][b][:], 0.0)
+
+        picked = keep.tile([P, PACK, S], BF16, name="picked")
+        for j in range(PACK - 1):
+            nc.vector.tensor_copy(picked[:, j, :], x_sb[j][:].indirect(offs_sb[:]))
+        j = PACK - 1
+        for d in range(TAPS):
+            nc.vector.tensor_copy(picked[:, j, d * V:(d + 1) * V],
+                                  x_sb[j][:].indirect(offs_sb[:, d * V // LIST:(d + 1) * V // LIST]))
+
+        x_codes, x_scales = [], []
+        w_codes = [[None] * BLOCKS for d in range(TAPS)]
+        w_scales = [[None] * BLOCKS for d in range(TAPS)]
+
+        def quantize(name, woven, width):
+            codes = keep.tile([P, width], U32, name=name + "_codes", align_bytes=64)
+            scales = keep.tile([P, width], U8, name=name + "_scales", align_bytes=64)
+            nc.vector.quantize_mx(out=codes[:].bitcast(FP8X4), scales=scales[:],
+                                  in_=woven[:].rearrange("p w j -> p (w j)"))
+            return codes, scales
+
+        def weave_x(d):
+            woven = keep.tile([P, V, PACK], BF16, name="x_woven%d" % d, align_bytes=64)
+            return woven
+
+        def weave_x_part(d, woven, lo, hi):
+            nc.scalar.copy(woven[:, lo:hi, :], picked[:, :, d * V + lo:d * V + hi].rearrange("p j v -> p v j"))
+
+        def weave_w(d, b, on_vector):
+            woven = keep.tile([P, P, PACK], BF16, name="w_woven%d_%d" % (d, b), align_bytes=64)
+            src = w_sb[d][:, :, b * P:(b + 1) * P].rearrange("p j n -> p n j")
+            if on_vector:
+                nc.vector.tensor_copy(woven[:], src)
+            else:
+                nc.scalar.copy(woven[:], src)
+            return woven
+
+        def product(d, b, xq, wq):
+            acc = psum.tile([P, V], F32, name="acc%d_%d" % (d, b))
+            nc.tensor.matmul_mx(out=acc[:], lhsT=wq[0][:].bitcast(FP8X4), lhsT_scale=wq[1][:],
+                                rhs=xq[0][:].bitcast(FP8X4), rhs_scale=xq[1][:], start=True, stop=True)
+            y = keep.tile([P, V], F32, name="y%d_%d" % (d, b))
+            nc.scalar.copy(y[:], acc[:])
+            return y
+
+        def scatter(d, b, y):
+            nc.vector.tensor_copy(cells[d][b][:].indirect(to_sb[d][:]), y[:])
+
+        def finish(b):
+            half = U // 2
+            for h in range(2):
+                cols = slice(h * half, (h + 1) * half)
+                total = keep.tile([P, half], F32, name="total%d_%d" % (b, h))
+                (nc.gpsimd if b == 0 else nc.vector).tensor_tensor(total[:], cells[0][b][:, cols], cells[1][b][:, cols], ADD)
+                res = keep.tile([P, half], F32, name="res%d_%d" % (b, h))
+                nc.scalar.activation(res[:], total[:], RELU)
+                nc.sync.dma_start(out[b * P:(b + 1) * P, cols], res[:])
+
+        xw0 = weave_x(0)
+        xw1 = weave_x(1)
+        weave_x_part(0, xw0, 0, V)
+        ww00 = weave_w(0, 0, True)
+        wq00 = quantize("w00", ww00, P)
+        xq0 = quantize("x0", xw0, V)
+        weave_x_part(1, xw1, 0, V // 2)
+        y00 = product(0, 0, xq0, wq00)
+        ww01 = weave_w(0, 1, True)
+        wq01 = quantize("w01", ww01, P)
+        scatter(0, 0, y00)
+        weave_x_part(1, xw1, V // 2, V)
+        ww10 = weave_w(1, 0, False)
+        xq1 = quantize("x1", xw1, V)
+        wq10 = quantize("w10", ww10, P)
+        y01 = product(0, 1, xq0, wq01)
+        scatter(0, 1, y01)
+        ww11 = weave_w(1, 1, False)
+        y10 = product(1, 0, xq1, wq10)
+        wq11 = quantize("w11", ww11, P)
+        y11 = product(1, 1, xq1, wq11)
+        scatter(1, 0, y10)
+        finish(0)
+        scatter(1, 1, y11)
+        finish(1)

@@ -44,15 +44,21 @@ def tile_picked_spconv_relu_e_kernel(tc, xT, w1, w2, offs, to1, to2, out):
         cells = [[keep.tile([P, U], F32, name="cells%d_%d" % (d, b)) for b in range(BLOCKS)] for d in range(TAPS)]
         for d in range(TAPS):
             for b in range(BLOCKS):
-                (nc.vector if d == 0 else nc.gpsimd).memset(cells[d][b][:], 0.0)
+                nc.vector.memset(cells[d][b][:], 0.0)
 
-        picked = keep.tile([P, PACK, S], BF16, name="picked")
+        stage = keep.tile([P, PACK * S - V + PACK * P], BF16, name="stage", align_bytes=64)
+        picked = stage[:, 0:PACK * S].rearrange("p (j s) -> p j s", j=PACK)
+        first_w = stage[:, PACK * S - V:].rearrange("p (n j) -> p n j", j=PACK)
         for j in range(PACK - 1):
             nc.vector.tensor_copy(picked[:, j, :], x_sb[j][:].indirect(offs_sb[:]))
-        j = PACK - 1
-        for d in range(TAPS):
+
+        def gather_last(d):
+            j = PACK - 1
             nc.vector.tensor_copy(picked[:, j, d * V:(d + 1) * V],
                                   x_sb[j][:].indirect(offs_sb[:, d * V // LIST:(d + 1) * V // LIST]))
+
+        def weave(copy, woven, planes):
+            copy(woven.rearrange("p (c i) j -> p c j i", i=PACK), planes.rearrange("p j (c i) -> p c j i", i=PACK))
 
         x_codes, x_scales = [], []
         w_codes = [[None] * BLOCKS for d in range(TAPS)]
@@ -62,24 +68,18 @@ def tile_picked_spconv_relu_e_kernel(tc, xT, w1, w2, offs, to1, to2, out):
             codes = keep.tile([P, width], U32, name=name + "_codes", align_bytes=64)
             scales = keep.tile([P, width], U8, name=name + "_scales", align_bytes=64)
             nc.vector.quantize_mx(out=codes[:].bitcast(FP8X4), scales=scales[:],
-                                  in_=woven[:].rearrange("p w j -> p (w j)"))
+                                  in_=woven.rearrange("p w j -> p (w j)"))
             return codes, scales
 
         def weave_x(d):
             woven = keep.tile([P, V, PACK], BF16, name="x_woven%d" % d, align_bytes=64)
-            return woven
+            weave(nc.scalar.copy, woven[:], picked[:, :, d * V:(d + 1) * V])
+            return woven[:]
 
-        def weave_x_part(d, woven, lo, hi):
-            nc.scalar.copy(woven[:, lo:hi, :], picked[:, :, d * V + lo:d * V + hi].rearrange("p j v -> p v j"))
-
-        def weave_w(d, b, on_vector):
+        def weave_w(d, b):
             woven = keep.tile([P, P, PACK], BF16, name="w_woven%d_%d" % (d, b), align_bytes=64)
-            src = w_sb[d][:, :, b * P:(b + 1) * P].rearrange("p j n -> p n j")
-            if on_vector:
-                nc.vector.tensor_copy(woven[:], src)
-            else:
-                nc.scalar.copy(woven[:], src)
-            return woven
+            weave(nc.scalar.copy, woven[:], w_sb[d][:, :, b * P:(b + 1) * P])
+            return woven[:]
 
         def product(d, b, xq, wq):
             acc = psum.tile([P, V], F32, name="acc%d_%d" % (d, b))
@@ -97,29 +97,31 @@ def tile_picked_spconv_relu_e_kernel(tc, xT, w1, w2, offs, to1, to2, out):
             for h in range(2):
                 cols = slice(h * half, (h + 1) * half)
                 total = keep.tile([P, half], F32, name="total%d_%d" % (b, h))
-                (nc.gpsimd if b == 0 else nc.vector).tensor_tensor(total[:], cells[0][b][:, cols], cells[1][b][:, cols], ADD)
+                nc.vector.tensor_tensor(total[:], cells[0][b][:, cols], cells[1][b][:, cols], ADD)
                 res = keep.tile([P, half], F32, name="res%d_%d" % (b, h))
-                nc.scalar.activation(res[:], total[:], RELU)
+                if b == BLOCKS - 1 and h == 1:
+                    nc.vector.tensor_scalar_max(res[:], total[:], 0.0)
+                else:
+                    nc.scalar.activation(res[:], total[:], RELU)
                 nc.sync.dma_start(out[b * P:(b + 1) * P, cols], res[:])
 
+        gather_last(0)
         xw0 = weave_x(0)
-        xw1 = weave_x(1)
-        weave_x_part(0, xw0, 0, V)
-        ww00 = weave_w(0, 0, True)
-        wq00 = quantize("w00", ww00, P)
+        weave(nc.vector.tensor_copy, first_w, w_sb[0][:, :, 0:P])
+        wq00 = quantize("w00", first_w, P)
         xq0 = quantize("x0", xw0, V)
-        weave_x_part(1, xw1, 0, V // 2)
+        gather_last(1)
+        ww01 = weave_w(0, 1)
         y00 = product(0, 0, xq0, wq00)
-        ww01 = weave_w(0, 1, True)
         wq01 = quantize("w01", ww01, P)
         scatter(0, 0, y00)
-        weave_x_part(1, xw1, V // 2, V)
-        ww10 = weave_w(1, 0, False)
+        xw1 = weave_x(1)
+        ww10 = weave_w(1, 0)
         xq1 = quantize("x1", xw1, V)
         wq10 = quantize("w10", ww10, P)
         y01 = product(0, 1, xq0, wq01)
         scatter(0, 1, y01)
-        ww11 = weave_w(1, 1, False)
+        ww11 = weave_w(1, 1)
         y10 = product(1, 0, xq1, wq10)
         wq11 = quantize("w11", ww11, P)
         y11 = product(1, 1, xq1, wq11)

@@ -13,12 +13,14 @@ U8 = mybir.dt.uint8
 FP8X4 = mybir.dt.float8_e4m3fn_x4
 ADD = mybir.AluOpType.add
 RELU = mybir.ActivationFunctionType.Relu
+COPY = mybir.ActivationFunctionType.Copy
 
 P = 128
 PACK = 4
 TAPS = 2
 BLOCKS = N // P
 LIST = 16
+HALF = V // 2
 
 
 def tile_picked_spconv_relu_e_kernel(tc, xT, w1, w2, offs, to1, to2, out):
@@ -31,15 +33,20 @@ def tile_picked_spconv_relu_e_kernel(tc, xT, w1, w2, offs, to1, to2, out):
         to_sb = [keep.tile([P, V // LIST], U16, name="to_sb%d" % d) for d in range(TAPS)]
         x_rows = xT.rearrange("(p j) t -> p j t", j=PACK)
         x_sb = [keep.tile([P, T], F32, name="x_sb%d" % j) for j in range(PACK)]
-        w_sb = [keep.tile([P, PACK, N], F32, name="w_sb%d" % d) for d in range(TAPS)]
+        w1_rows = w1.rearrange("(p j) n -> p j n", j=PACK)
+        w1_sb = [keep.tile([P, PACK, P], F32, name="w1_sb%d" % b) for b in range(BLOCKS)]
+        w2_sb = keep.tile([P, PACK, N], F32, name="w2_sb")
+        w_sb = [[w1_sb[0][:], w1_sb[1][:]], [w2_sb[:, :, 0:P], w2_sb[:, :, P:N]]]
 
         nc.sync.dma_start(x_sb[0][:], x_rows[:, 0, :])
         nc.sync.dma_start(offs_sb[:], offs)
         for j in range(1, PACK):
             nc.sync.dma_start(x_sb[j][:], x_rows[:, j, :])
-        for d, (w, to) in enumerate(((w1, to1), (w2, to2))):
-            nc.sync.dma_start(w_sb[d][:], w.rearrange("(p j) n -> p j n", j=PACK))
-            nc.sync.dma_start(to_sb[d][:], to)
+        for b in range(BLOCKS):
+            nc.sync.dma_start(w1_sb[b][:], w1_rows[:, :, b * P:(b + 1) * P])
+        nc.sync.dma_start(to_sb[0][:], to1)
+        nc.sync.dma_start(w2_sb[:], w2.rearrange("(p j) n -> p j n", j=PACK))
+        nc.sync.dma_start(to_sb[1][:], to2)
 
         cells = [[keep.tile([P, U], F32, name="cells%d_%d" % (d, b)) for b in range(BLOCKS)] for d in range(TAPS)]
         for d in range(TAPS):
@@ -48,84 +55,95 @@ def tile_picked_spconv_relu_e_kernel(tc, xT, w1, w2, offs, to1, to2, out):
 
         stage = keep.tile([P, PACK * S - V + PACK * P], BF16, name="stage", align_bytes=64)
         picked = stage[:, 0:PACK * S].rearrange("p (j s) -> p j s", j=PACK)
-        first_w = stage[:, PACK * S - V:].rearrange("p (n j) -> p n j", j=PACK)
-        for j in range(PACK - 1):
-            nc.vector.tensor_copy(picked[:, j, :], x_sb[j][:].indirect(offs_sb[:]))
+        first_t = keep.tile([P, P, PACK], BF16, name="first_t", align_bytes=64)
+        first_w = first_t[:]
 
-        def gather_last(d):
-            j = PACK - 1
-            nc.vector.tensor_copy(picked[:, j, d * V:(d + 1) * V],
-                                  x_sb[j][:].indirect(offs_sb[:, d * V // LIST:(d + 1) * V // LIST]))
+        def entries(lists, lo, hi):
+            return lists[:, lo // LIST:hi // LIST]
+
+        def gather(j, lo, hi):
+            nc.vector.tensor_copy(picked[:, j, lo:hi], x_sb[j][:].indirect(entries(offs_sb, lo, hi)))
+
+        def gather_on_scalar(j, lo, hi):
+            rounded = keep.tile([P, T], BF16, name="rounded%d" % j)
+            nc.scalar.copy(rounded[:], x_sb[j][:])
+            nc.scalar.activation(picked[:, j, lo:hi], rounded[:].indirect(entries(offs_sb, lo, hi)), COPY)
 
         def weave(copy, woven, planes):
             copy(woven.rearrange("p (c i) j -> p c j i", i=PACK), planes.rearrange("p j (c i) -> p c j i", i=PACK))
-
-        x_codes, x_scales = [], []
-        w_codes = [[None] * BLOCKS for d in range(TAPS)]
-        w_scales = [[None] * BLOCKS for d in range(TAPS)]
 
         def quantize(name, woven, width):
             codes = keep.tile([P, width], U32, name=name + "_codes", align_bytes=64)
             scales = keep.tile([P, width], U8, name=name + "_scales", align_bytes=64)
             nc.vector.quantize_mx(out=codes[:].bitcast(FP8X4), scales=scales[:],
                                   in_=woven.rearrange("p w j -> p (w j)"))
-            return codes, scales
+            return codes[:], scales[:]
 
-        def weave_x(d):
-            woven = keep.tile([P, V, PACK], BF16, name="x_woven%d" % d, align_bytes=64)
-            weave(nc.scalar.copy, woven[:], picked[:, :, d * V:(d + 1) * V])
-            return woven[:]
-
-        def weave_w(d, b):
+        def weave_w(d, b, copy):
             woven = keep.tile([P, P, PACK], BF16, name="w_woven%d_%d" % (d, b), align_bytes=64)
-            weave(nc.scalar.copy, woven[:], w_sb[d][:, :, b * P:(b + 1) * P])
+            weave(copy, woven[:], w_sb[d][b])
             return woven[:]
 
-        def product(d, b, xq, wq):
-            acc = psum.tile([P, V], F32, name="acc%d_%d" % (d, b))
-            nc.tensor.matmul_mx(out=acc[:], lhsT=wq[0][:].bitcast(FP8X4), lhsT_scale=wq[1][:],
-                                rhs=xq[0][:].bitcast(FP8X4), rhs_scale=xq[1][:], start=True, stop=True)
-            y = keep.tile([P, V], F32, name="y%d_%d" % (d, b))
-            nc.scalar.copy(y[:], acc[:])
-            return y
+        accs = [[psum.tile([P, V], F32, name="acc%d_%d" % (d, b)) for b in range(BLOCKS)] for d in range(TAPS)]
 
-        def scatter(d, b, y):
-            nc.vector.tensor_copy(cells[d][b][:].indirect(to_sb[d][:]), y[:])
+        def multiply(acc, xq, wq):
+            nc.tensor.matmul_mx(out=acc, lhsT=wq[0].bitcast(FP8X4), lhsT_scale=wq[1],
+                                rhs=xq[0].bitcast(FP8X4), rhs_scale=xq[1], start=True, stop=True)
 
-        def finish(b):
-            half = U // 2
-            for h in range(2):
-                cols = slice(h * half, (h + 1) * half)
-                total = keep.tile([P, half], F32, name="total%d_%d" % (b, h))
-                nc.vector.tensor_tensor(total[:], cells[0][b][:, cols], cells[1][b][:, cols], ADD)
-                res = keep.tile([P, half], F32, name="res%d_%d" % (b, h))
-                if b == BLOCKS - 1 and h == 1:
-                    nc.vector.tensor_scalar_max(res[:], total[:], 0.0)
-                else:
-                    nc.scalar.activation(res[:], total[:], RELU)
+        def leave(name, acc):
+            y = keep.tile([P, acc.shape[1]], F32, name=name)
+            nc.scalar.copy(y[:], acc)
+            return y[:]
+
+        def scatter(d, b, lo, hi, y):
+            nc.vector.tensor_copy(cells[d][b][:].indirect(entries(to_sb[d], lo, hi)), y)
+
+        def finish(b, cuts, engines):
+            for h in range(len(cuts) - 1):
+                cols = slice(cuts[h], cuts[h + 1])
+                width = cuts[h + 1] - cuts[h]
+                total = keep.tile([P, width], F32, name="total%d_%d" % (b, cuts[h]))
+                engines[h].tensor_tensor(total[:], cells[0][b][:, cols], cells[1][b][:, cols], ADD)
+                res = keep.tile([P, width], F32, name="res%d_%d" % (b, cuts[h]))
+                nc.scalar.activation(res[:], total[:], RELU)
                 nc.sync.dma_start(out[b * P:(b + 1) * P, cols], res[:])
 
-        gather_last(0)
-        xw0 = weave_x(0)
-        weave(nc.vector.tensor_copy, first_w, w_sb[0][:, :, 0:P])
+        x_woven = [keep.tile([P, V, PACK], BF16, name="x_woven%d" % d, align_bytes=64) for d in range(TAPS)]
+
+        def weave_pair(d, j):
+            weave(nc.scalar.copy, x_woven[d][:, :, j:j + 2], picked[:, j:j + 2, d * V:(d + 1) * V])
+
+        gather(0, 0, V)
+        gather_on_scalar(0, V, S)
+        gather(1, 0, S)
+        weave_pair(0, 0)
+        weave_pair(1, 0)
+        gather(2, 0, S)
+        gather(3, 0, V)
+        gather(3, V, S)
+        weave_pair(0, 2)
+        weave(nc.vector.tensor_copy, first_w, w_sb[0][0])
+        xq0 = quantize("x0", x_woven[0][:], V)
         wq00 = quantize("w00", first_w, P)
-        xq0 = quantize("x0", xw0, V)
-        gather_last(1)
-        ww01 = weave_w(0, 1)
-        y00 = product(0, 0, xq0, wq00)
+        multiply(accs[0][0][:], xq0, wq00)
+        weave_pair(1, 2)
+        xq1 = quantize("x1", x_woven[1][:], V)
+        ww01 = weave_w(0, 1, nc.scalar.copy)
         wq01 = quantize("w01", ww01, P)
-        scatter(0, 0, y00)
-        xw1 = weave_x(1)
-        ww10 = weave_w(1, 0)
-        xq1 = quantize("x1", xw1, V)
-        wq10 = quantize("w10", ww10, P)
-        y01 = product(0, 1, xq0, wq01)
-        scatter(0, 1, y01)
-        ww11 = weave_w(1, 1)
-        y10 = product(1, 0, xq1, wq10)
-        wq11 = quantize("w11", ww11, P)
-        y11 = product(1, 1, xq1, wq11)
-        scatter(1, 0, y10)
-        finish(0)
-        scatter(1, 1, y11)
-        finish(1)
+        y00 = leave("y00", accs[0][0][:])
+        scatter(0, 0, 0, V, y00)
+        multiply(accs[0][1][:], xq0, wq01)
+        ww1 = keep.tile([P, N, PACK], BF16, name="ww1", align_bytes=64)
+        weave(nc.scalar.copy, ww1[:], w2_sb[:])
+        wq1 = quantize("w1", ww1[:], N)
+        y01 = w2_sb[:, 0, :]
+        nc.scalar.copy(y01, accs[0][1][:])
+        scatter(0, 1, 0, V, y01)
+        for b in range(BLOCKS):
+            multiply(accs[1][b][:], xq1, (wq1[0][:, b * P:(b + 1) * P], wq1[1][:, b * P:(b + 1) * P]))
+        y10 = leave("y10", accs[1][0][:])
+        y11 = leave("y11", accs[1][1][:])
+        scatter(1, 0, 0, V, y10)
+        scatter(1, 1, 0, V, y11)
+        finish(0, [0, 256, 512], [nc.gpsimd, nc.gpsimd])
+        finish(1, [0, 256, 512], [nc.vector, nc.vector])

@@ -12,6 +12,8 @@ U16 = mybir.dt.uint16
 U8 = mybir.dt.uint8
 FP8X4 = mybir.dt.float8_e4m3fn_x4
 ADD = mybir.AluOpType.add
+MULT = mybir.AluOpType.mult
+MAX = mybir.AluOpType.max
 RELU = mybir.ActivationFunctionType.Relu
 COPY = mybir.ActivationFunctionType.Copy
 
@@ -20,7 +22,6 @@ PACK = 4
 TAPS = 2
 BLOCKS = N // P
 LIST = 16
-HALF = V // 2
 
 
 def tile_picked_spconv_relu_e_kernel(tc, xT, w1, w2, offs, to1, to2, out):
@@ -33,41 +34,34 @@ def tile_picked_spconv_relu_e_kernel(tc, xT, w1, w2, offs, to1, to2, out):
         to_sb = [keep.tile([P, V // LIST], U16, name="to_sb%d" % d) for d in range(TAPS)]
         x_rows = xT.rearrange("(p j) t -> p j t", j=PACK)
         x_sb = [keep.tile([P, T], F32, name="x_sb%d" % j) for j in range(PACK)]
-        w1_rows = w1.rearrange("(p j) n -> p j n", j=PACK)
-        w1_sb = [keep.tile([P, PACK, P], F32, name="w1_sb%d" % b) for b in range(BLOCKS)]
-        w2_sb = keep.tile([P, PACK, N], F32, name="w2_sb")
-        w_sb = [[w1_sb[0][:], w1_sb[1][:]], [w2_sb[:, :, 0:P], w2_sb[:, :, P:N]]]
+        w_sb = [keep.tile([P, PACK, N], F32, name="w_sb%d" % d) for d in range(TAPS)]
 
         nc.sync.dma_start(x_sb[0][:], x_rows[:, 0, :])
         nc.sync.dma_start(offs_sb[:], offs)
-        for j in range(1, PACK):
-            nc.sync.dma_start(x_sb[j][:], x_rows[:, j, :])
-        for b in range(BLOCKS):
-            nc.sync.dma_start(w1_sb[b][:], w1_rows[:, :, b * P:(b + 1) * P])
+        nc.sync.dma_start(x_sb[1][:], x_rows[:, 1, :])
+        nc.sync.dma_start(x_sb[2][:], x_rows[:, 2, :])
+        nc.sync.dma_start(x_sb[3][:], x_rows[:, 3, :])
+        nc.sync.dma_start(w_sb[0][:], w1.rearrange("(p j) n -> p j n", j=PACK))
+        nc.sync.dma_start(w_sb[1][:], w2.rearrange("(p j) n -> p j n", j=PACK))
         nc.sync.dma_start(to_sb[0][:], to1)
-        nc.sync.dma_start(w2_sb[:], w2.rearrange("(p j) n -> p j n", j=PACK))
         nc.sync.dma_start(to_sb[1][:], to2)
 
         cells = [[keep.tile([P, U], F32, name="cells%d_%d" % (d, b)) for b in range(BLOCKS)] for d in range(TAPS)]
-        for d in range(TAPS):
-            for b in range(BLOCKS):
-                nc.vector.memset(cells[d][b][:], 0.0)
-
-        stage = keep.tile([P, PACK * S - V + PACK * P], BF16, name="stage", align_bytes=64)
-        picked = stage[:, 0:PACK * S].rearrange("p (j s) -> p j s", j=PACK)
-        first_t = keep.tile([P, P, PACK], BF16, name="first_t", align_bytes=64)
-        first_w = first_t[:]
+        for b in range(BLOCKS):
+            nc.vector.memset(cells[1][b][:], 0.0)
+            nc.scalar.copy(cells[0][b][:], cells[1][b][:])
 
         def entries(lists, lo, hi):
             return lists[:, lo // LIST:hi // LIST]
 
-        def gather(j, lo, hi):
-            nc.vector.tensor_copy(picked[:, j, lo:hi], x_sb[j][:].indirect(entries(offs_sb, lo, hi)))
+        x_woven = [keep.tile([P, V, PACK], BF16, name="x_woven%d" % d, align_bytes=64) for d in range(TAPS)]
+        pairs = [keep.tile([P, 2, V], BF16, name="pairs%d" % h) for h in range(2)]
 
-        def gather_on_scalar(j, lo, hi):
-            rounded = keep.tile([P, T], BF16, name="rounded%d" % j)
-            nc.scalar.copy(rounded[:], x_sb[j][:])
-            nc.scalar.activation(picked[:, j, lo:hi], rounded[:].indirect(entries(offs_sb, lo, hi)), COPY)
+        def gather0(j):
+            nc.vector.tensor_copy(x_woven[0][:, :, j], x_sb[j][:].indirect(entries(offs_sb, 0, V)))
+
+        def gather1(j):
+            nc.scalar.activation(pairs[j // 2][:, j % 2, :], x_sb[j][:].indirect(entries(offs_sb, V, S)), COPY)
 
         def weave(copy, woven, planes):
             copy(woven.rearrange("p (c i) j -> p c j i", i=PACK), planes.rearrange("p j (c i) -> p c j i", i=PACK))
@@ -79,71 +73,71 @@ def tile_picked_spconv_relu_e_kernel(tc, xT, w1, w2, offs, to1, to2, out):
                                   in_=woven.rearrange("p w j -> p (w j)"))
             return codes[:], scales[:]
 
-        def weave_w(d, b, copy):
-            woven = keep.tile([P, P, PACK], BF16, name="w_woven%d_%d" % (d, b), align_bytes=64)
-            weave(copy, woven[:], w_sb[d][b])
-            return woven[:]
-
         accs = [[psum.tile([P, V], F32, name="acc%d_%d" % (d, b)) for b in range(BLOCKS)] for d in range(TAPS)]
 
         def multiply(acc, xq, wq):
-            nc.tensor.matmul_mx(out=acc, lhsT=wq[0].bitcast(FP8X4), lhsT_scale=wq[1],
+            nc.tensor.matmul_mx(out=acc[:], lhsT=wq[0].bitcast(FP8X4), lhsT_scale=wq[1],
                                 rhs=xq[0].bitcast(FP8X4), rhs_scale=xq[1], start=True, stop=True)
 
-        def leave(name, acc):
-            y = keep.tile([P, acc.shape[1]], F32, name=name)
-            nc.scalar.copy(y[:], acc)
+        def leave(copy, d, b):
+            y = keep.tile([P, V], F32, name="y%d_%d" % (d, b))
+            copy(y[:], accs[d][b][:])
             return y[:]
 
-        def scatter(d, b, lo, hi, y):
-            nc.vector.tensor_copy(cells[d][b][:].indirect(entries(to_sb[d], lo, hi)), y)
+        def scatter_v(d, b, y):
+            nc.vector.tensor_copy(cells[d][b][:].indirect(to_sb[d][:]), y)
 
-        def finish(b, cuts, engines):
-            for h in range(len(cuts) - 1):
-                cols = slice(cuts[h], cuts[h + 1])
-                width = cuts[h + 1] - cuts[h]
-                total = keep.tile([P, width], F32, name="total%d_%d" % (b, cuts[h]))
-                engines[h].tensor_tensor(total[:], cells[0][b][:, cols], cells[1][b][:, cols], ADD)
-                res = keep.tile([P, width], F32, name="res%d_%d" % (b, cuts[h]))
-                nc.scalar.activation(res[:], total[:], RELU)
-                nc.sync.dma_start(out[b * P:(b + 1) * P, cols], res[:])
+        def scatter_s(d, b, y):
+            nc.scalar.activation(cells[d][b][:].indirect(to_sb[d][:]), y, COPY)
 
-        x_woven = [keep.tile([P, V, PACK], BF16, name="x_woven%d" % d, align_bytes=64) for d in range(TAPS)]
+        def relu_s(res, total):
+            nc.scalar.activation(res, total, RELU)
 
-        def weave_pair(d, j):
-            weave(nc.scalar.copy, x_woven[d][:, :, j:j + 2], picked[:, j:j + 2, d * V:(d + 1) * V])
+        def relu_v(res, total):
+            nc.vector.tensor_scalar_max(res, total, 0.0)
 
-        gather(0, 0, V)
-        gather_on_scalar(0, V, S)
-        gather(1, 0, S)
-        weave_pair(0, 0)
-        weave_pair(1, 0)
-        gather(2, 0, S)
-        gather(3, 0, V)
-        gather(3, V, S)
-        weave_pair(0, 2)
-        weave(nc.vector.tensor_copy, first_w, w_sb[0][0])
+        def relu_g(res, total):
+            nc.gpsimd.tensor_scalar(res, total, 1.0, 0.0, MULT, MAX)
+
+        def finish(b, lo, hi, adder, relu):
+            total = keep.tile([P, hi - lo], F32, name="total%d_%d" % (b, lo))
+            adder.tensor_tensor(total[:], cells[0][b][:, lo:hi], cells[1][b][:, lo:hi], ADD)
+            res = keep.tile([P, hi - lo], F32, name="res%d_%d" % (b, lo))
+            relu(res[:], total[:])
+            nc.sync.dma_start(out[b * P:(b + 1) * P, lo:hi], res[:])
+
+        def weave_w(copy, d, b):
+            woven = keep.tile([P, P, PACK], BF16, name="w_woven%d_%d" % (d, b), align_bytes=64)
+            weave(copy, woven[:], w_sb[d][:, :, b * P:(b + 1) * P])
+            return woven[:]
+
+        for j in range(2):
+            gather0(j)
+            gather1(j)
+        weave(nc.vector.tensor_copy, x_woven[1][:, :, 0:2], pairs[0][:])
+        for j in range(2, PACK):
+            gather0(j)
+            gather1(j)
         xq0 = quantize("x0", x_woven[0][:], V)
-        wq00 = quantize("w00", first_w, P)
-        multiply(accs[0][0][:], xq0, wq00)
-        weave_pair(1, 2)
+        weave(nc.vector.tensor_copy, x_woven[1][:, :, 2:4], pairs[1][:])
+        ww00 = weave_w(nc.scalar.copy, 0, 0)
+        ww01 = weave_w(nc.scalar.copy, 0, 1)
         xq1 = quantize("x1", x_woven[1][:], V)
-        ww01 = weave_w(0, 1, nc.scalar.copy)
-        wq01 = quantize("w01", ww01, P)
-        y00 = leave("y00", accs[0][0][:])
-        scatter(0, 0, 0, V, y00)
-        multiply(accs[0][1][:], xq0, wq01)
-        ww1 = keep.tile([P, N, PACK], BF16, name="ww1", align_bytes=64)
-        weave(nc.scalar.copy, ww1[:], w2_sb[:])
-        wq1 = quantize("w1", ww1[:], N)
-        y01 = w2_sb[:, 0, :]
-        nc.scalar.copy(y01, accs[0][1][:])
-        scatter(0, 1, 0, V, y01)
-        for b in range(BLOCKS):
-            multiply(accs[1][b][:], xq1, (wq1[0][:, b * P:(b + 1) * P], wq1[1][:, b * P:(b + 1) * P]))
-        y10 = leave("y10", accs[1][0][:])
-        y11 = leave("y11", accs[1][1][:])
-        scatter(1, 0, 0, V, y10)
-        scatter(1, 1, 0, V, y11)
-        finish(0, [0, 256, 512], [nc.gpsimd, nc.gpsimd])
-        finish(1, [0, 256, 512], [nc.vector, nc.vector])
+        multiply(accs[0][0], xq0, quantize("w00", ww00, P))
+        ww10 = weave_w(nc.vector.tensor_copy, 1, 0)
+        multiply(accs[0][1], xq0, quantize("w01", ww01, P))
+        multiply(accs[1][0], xq1, quantize("w10", ww10, P))
+        ww11 = weave_w(nc.vector.tensor_copy, 1, 1)
+        y00 = leave(nc.scalar.copy, 0, 0)
+        scatter_s(0, 0, y00)
+        y10 = leave(nc.vector.tensor_copy, 1, 0)
+        multiply(accs[1][1], xq1, quantize("w11", ww11, P))
+        scatter_v(1, 0, y10)
+        y01 = leave(nc.scalar.copy, 0, 1)
+        scatter_s(0, 1, y01)
+        y11 = leave(nc.vector.tensor_copy, 1, 1)
+        scatter_v(1, 1, y11)
+        finish(0, 0, 256, nc.gpsimd, relu_s)
+        finish(0, 256, U, nc.gpsimd, relu_s)
+        finish(1, 0, 256, nc.vector, relu_v)
+        finish(1, 256, U, nc.vector, relu_v)

@@ -22,6 +22,7 @@ PACK = 4
 TAPS = 2
 BLOCKS = N // P
 LIST = 16
+CUTS = [(0, 256), (256, 512)]
 
 
 def tile_picked_spconv_relu_e_kernel(tc, xT, w1, w2, offs, to1, to2, out):
@@ -73,16 +74,17 @@ def tile_picked_spconv_relu_e_kernel(tc, xT, w1, w2, offs, to1, to2, out):
                                   in_=woven.rearrange("p w j -> p (w j)"))
             return codes[:], scales[:]
 
-        accs = [[psum.tile([P, V], F32, name="acc%d_%d" % (d, b)) for b in range(BLOCKS)] for d in range(TAPS)]
+        first = [psum.tile([P, V], F32, name="first%d" % d) for d in range(TAPS)]
+        second = [psum.tile([P, V], F32, name="second%d" % d) for d in range(TAPS)]
 
         def multiply(acc, xq, wq):
-            nc.tensor.matmul_mx(out=acc[:], lhsT=wq[0].bitcast(FP8X4), lhsT_scale=wq[1],
+            nc.tensor.matmul_mx(out=acc, lhsT=wq[0].bitcast(FP8X4), lhsT_scale=wq[1],
                                 rhs=xq[0].bitcast(FP8X4), rhs_scale=xq[1], start=True, stop=True)
 
-        def leave(copy, d, b):
-            y = keep.tile([P, V], F32, name="y%d_%d" % (d, b))
-            copy(y[:], accs[d][b][:])
-            return y[:]
+        def leave(copy, name, acc):
+            y = keep.tile([P, acc.shape[1]], F32, name=name)
+            copy(y[:], acc)
+            return y
 
         def scatter_v(d, b, y):
             nc.vector.tensor_copy(cells[d][b][:].indirect(to_sb[d][:]), y)
@@ -99,12 +101,18 @@ def tile_picked_spconv_relu_e_kernel(tc, xT, w1, w2, offs, to1, to2, out):
         def relu_g(res, total):
             nc.gpsimd.tensor_scalar(res, total, 1.0, 0.0, MULT, MAX)
 
-        def finish(b, lo, hi, adder, relu):
+        def add(b, lo, hi, adder):
             total = keep.tile([P, hi - lo], F32, name="total%d_%d" % (b, lo))
             adder.tensor_tensor(total[:], cells[0][b][:, lo:hi], cells[1][b][:, lo:hi], ADD)
+            return total
+
+        def store(b, lo, hi, total, relu):
             res = keep.tile([P, hi - lo], F32, name="res%d_%d" % (b, lo))
             relu(res[:], total[:])
-            nc.sync.dma_start(out[b * P:(b + 1) * P, lo:hi], res[:])
+            [nc.scalar, nc.sync][b].dma_start(out[b * P:(b + 1) * P, lo:hi], res[:])
+
+        def finish(b, lo, hi, adder, relu):
+            store(b, lo, hi, add(b, lo, hi, adder), relu)
 
         def weave_w(copy, d, b):
             woven = keep.tile([P, P, PACK], BF16, name="w_woven%d_%d" % (d, b), align_bytes=64)
@@ -118,26 +126,28 @@ def tile_picked_spconv_relu_e_kernel(tc, xT, w1, w2, offs, to1, to2, out):
         for j in range(2, PACK):
             gather0(j)
             gather1(j)
-        xq0 = quantize("x0", x_woven[0][:], V)
         weave(nc.vector.tensor_copy, x_woven[1][:, :, 2:4], pairs[1][:])
+        xq0 = quantize("x0", x_woven[0][:], V)
+        xq1 = quantize("x1", x_woven[1][:], V)
         ww00 = weave_w(nc.scalar.copy, 0, 0)
         ww01 = weave_w(nc.scalar.copy, 0, 1)
-        xq1 = quantize("x1", x_woven[1][:], V)
-        multiply(accs[0][0], xq0, quantize("w00", ww00, P))
+        ww11 = weave_w(nc.scalar.copy, 1, 1)
+        multiply(first[0][:], xq0, quantize("w00", ww00, P))
         ww10 = weave_w(nc.vector.tensor_copy, 1, 0)
-        multiply(accs[0][1], xq0, quantize("w01", ww01, P))
-        multiply(accs[1][0], xq1, quantize("w10", ww10, P))
-        ww11 = weave_w(nc.vector.tensor_copy, 1, 1)
-        y00 = leave(nc.scalar.copy, 0, 0)
-        scatter_s(0, 0, y00)
-        y10 = leave(nc.vector.tensor_copy, 1, 0)
-        multiply(accs[1][1], xq1, quantize("w11", ww11, P))
-        scatter_v(1, 0, y10)
-        y01 = leave(nc.scalar.copy, 0, 1)
-        scatter_s(0, 1, y01)
-        y11 = leave(nc.vector.tensor_copy, 1, 1)
-        scatter_v(1, 1, y11)
+        wq01 = quantize("w01", ww01, P)
+        multiply(first[1][:], xq1, quantize("w10", ww10, P))
+        multiply(second[0][:], xq0, wq01)
+        multiply(second[1][:], xq1, quantize("w11", ww11, P))
+        y00 = leave(nc.scalar.copy, "y00", first[0][:])
+        scatter_s(0, 0, y00[:])
+        y10 = leave(nc.vector.tensor_copy, "y10", first[1][:])
+        y01 = leave(nc.vector.tensor_copy, "y01", second[0][:])
+        scatter_v(1, 0, y10[:])
+        y11 = leave(nc.scalar.copy, "y11", second[1][:])
+        scatter_s(0, 1, y01[:])
+        scatter_v(1, 1, y11[:])
         finish(0, 0, 256, nc.gpsimd, relu_s)
         finish(0, 256, U, nc.gpsimd, relu_s)
-        finish(1, 0, 256, nc.vector, relu_v)
-        finish(1, 256, U, nc.vector, relu_v)
+        totals = [add(1, lo, hi, nc.vector) for lo, hi in CUTS]
+        for h, relu in enumerate([relu_v, relu_v]):
+            store(1, CUTS[h][0], CUTS[h][1], totals[h], relu)

@@ -35,15 +35,17 @@ def tile_picked_spconv_relu_e_kernel(tc, xT, w1, w2, offs, to1, to2, out):
         to_sb = [keep.tile([P, V // LIST], U16, name="to_sb%d" % d) for d in range(TAPS)]
         x_rows = xT.rearrange("(p j) t -> p j t", j=PACK)
         x_sb = [keep.tile([P, T], F32, name="x_sb%d" % j) for j in range(PACK)]
-        w_sb = [keep.tile([P, PACK, N], F32, name="w_sb%d" % d) for d in range(TAPS)]
+        w_rows = [w.rearrange("(p j) n -> p j n", j=PACK) for w in (w1, w2)]
+        w_sb = [[keep.tile([P, PACK, P], F32, name="w_sb%d_%d" % (d, b), tag="w_sb%d_%d" % (d, b), align_bytes=64) for b in range(BLOCKS)] for d in range(TAPS)]
 
         nc.sync.dma_start(x_sb[0][:], x_rows[:, 0, :])
         nc.sync.dma_start(offs_sb[:], offs)
         nc.sync.dma_start(x_sb[1][:], x_rows[:, 1, :])
         nc.sync.dma_start(x_sb[2][:], x_rows[:, 2, :])
         nc.sync.dma_start(x_sb[3][:], x_rows[:, 3, :])
-        nc.sync.dma_start(w_sb[0][:], w1.rearrange("(p j) n -> p j n", j=PACK))
-        nc.sync.dma_start(w_sb[1][:], w2.rearrange("(p j) n -> p j n", j=PACK))
+        for b in range(BLOCKS):
+            for d in range(TAPS):
+                nc.sync.dma_start(w_sb[d][b][:], w_rows[d][:, :, b * P:(b + 1) * P])
         nc.sync.dma_start(to_sb[0][:], to1)
         nc.sync.dma_start(to_sb[1][:], to2)
 
@@ -67,8 +69,8 @@ def tile_picked_spconv_relu_e_kernel(tc, xT, w1, w2, offs, to1, to2, out):
         def weave(copy, woven, planes):
             copy(woven.rearrange("p (c i) j -> p c j i", i=PACK), planes.rearrange("p j (c i) -> p c j i", i=PACK))
 
-        def quantize(name, woven, width):
-            codes = keep.tile([P, width], U32, name=name + "_codes", align_bytes=64)
+        def quantize(name, woven, width, tag=None):
+            codes = keep.tile([P, width], U32, name=name + "_codes", tag=tag or name, align_bytes=64)
             scales = keep.tile([P, width], U8, name=name + "_scales", align_bytes=64)
             nc.vector.quantize_mx(out=codes[:].bitcast(FP8X4), scales=scales[:],
                                   in_=woven.rearrange("p w j -> p (w j)"))
@@ -81,8 +83,8 @@ def tile_picked_spconv_relu_e_kernel(tc, xT, w1, w2, offs, to1, to2, out):
             nc.tensor.matmul_mx(out=acc, lhsT=wq[0].bitcast(FP8X4), lhsT_scale=wq[1],
                                 rhs=xq[0].bitcast(FP8X4), rhs_scale=xq[1], start=True, stop=True)
 
-        def leave(copy, name, acc):
-            y = keep.tile([P, acc.shape[1]], F32, name=name)
+        def leave(copy, name, acc, tag=None):
+            y = keep.tile([P, acc.shape[1]], F32, name=name, tag=tag or name, align_bytes=64)
             copy(y[:], acc)
             return y
 
@@ -115,8 +117,8 @@ def tile_picked_spconv_relu_e_kernel(tc, xT, w1, w2, offs, to1, to2, out):
             store(b, lo, hi, add(b, lo, hi, adder), relu)
 
         def weave_w(copy, d, b):
-            woven = keep.tile([P, P, PACK], BF16, name="w_woven%d_%d" % (d, b), align_bytes=64)
-            weave(copy, woven[:], w_sb[d][:, :, b * P:(b + 1) * P])
+            woven = keep.tile([P, P, PACK], BF16, name="w_woven%d_%d" % (d, b), tag="w_woven%d_%d" % (d, b), align_bytes=64)
+            weave(copy, woven[:], w_sb[d][b][:])
             return woven[:]
 
         for j in range(2):
@@ -128,22 +130,21 @@ def tile_picked_spconv_relu_e_kernel(tc, xT, w1, w2, offs, to1, to2, out):
             gather1(j)
         weave(nc.vector.tensor_copy, x_woven[1][:, :, 2:4], pairs[1][:])
         xq0 = quantize("x0", x_woven[0][:], V)
-        xq1 = quantize("x1", x_woven[1][:], V)
-        ww00 = weave_w(nc.scalar.copy, 0, 0)
-        ww01 = weave_w(nc.scalar.copy, 0, 1)
-        ww11 = weave_w(nc.scalar.copy, 1, 1)
-        multiply(first[0][:], xq0, quantize("w00", ww00, P))
-        ww10 = weave_w(nc.vector.tensor_copy, 1, 0)
-        wq01 = quantize("w01", ww01, P)
-        multiply(first[1][:], xq1, quantize("w10", ww10, P))
-        multiply(second[0][:], xq0, wq01)
-        multiply(second[1][:], xq1, quantize("w11", ww11, P))
-        y00 = leave(nc.scalar.copy, "y00", first[0][:])
-        scatter_s(0, 0, y00[:])
+        ww = [[None, None], [None, None]]
+        for b in range(BLOCKS):
+            for d in range(TAPS):
+                ww[d][b] = weave_w(nc.scalar.copy, d, b)
+        multiply(first[0][:], xq0, quantize("w00", ww[0][0], P))
+        xq1 = quantize("x1", x_woven[1][:], V, "w_sb0_0")
+        multiply(first[1][:], xq1, quantize("w10", ww[1][0], P))
+        y00 = leave(nc.vector.tensor_copy, "y00", first[0][:], "w_woven1_0")
+        multiply(second[0][:], xq0, quantize("w01", ww[0][1], P))
         y10 = leave(nc.vector.tensor_copy, "y10", first[1][:])
-        y01 = leave(nc.vector.tensor_copy, "y01", second[0][:])
+        multiply(second[1][:], xq1, quantize("w11", ww[1][1], P))
+        scatter_s(0, 0, y00[:])
         scatter_v(1, 0, y10[:])
         y11 = leave(nc.scalar.copy, "y11", second[1][:])
+        y01 = leave(nc.scalar.copy, "y01", second[0][:])
         scatter_s(0, 1, y01[:])
         scatter_v(1, 1, y11[:])
         finish(0, 0, 256, nc.gpsimd, relu_s)

@@ -67,7 +67,7 @@ def tile_picked_spconv_relu_e_kernel(tc, xT, w1, w2, offs, to1, to2, out):
             nc.scalar.activation(pairs[j // 2][:, j % 2, :], x_sb[j][:].indirect(entries(offs_sb, V, S)), COPY)
 
         def weave(copy, woven, planes):
-            copy(woven.rearrange("p (c i) j -> p c j i", i=PACK), planes.rearrange("p j (c i) -> p c j i", i=PACK))
+            copy(woven.rearrange("p (c i) j -> p c j i", i=2), planes.rearrange("p j (c i) -> p c j i", i=2))
 
         def quantize(name, woven, width, tag=None):
             codes = keep.tile([P, width], U32, name=name + "_codes", tag=tag or name, align_bytes=64)

@@ -22,6 +22,7 @@ PACK = 4
 TAPS = 2
 BLOCKS = N // P
 LIST = 16
+HALF = V // 2
 CUTS = [(0, 256), (256, 512)]
 
 
@@ -124,7 +125,8 @@ def tile_picked_spconv_relu_e_kernel(tc, xT, w1, w2, offs, to1, to2, out):
         for j in range(2):
             gather0(j)
             gather1(j)
-        weave(nc.vector.tensor_copy, x_woven[1][:, :, 0:2], pairs[0][:])
+        weave(nc.vector.tensor_copy, x_woven[1][:, 0:HALF, 0:2], pairs[0][:, :, 0:HALF])
+        weave(nc.scalar.copy, x_woven[1][:, HALF:V, 0:2], pairs[0][:, :, HALF:V])
         for j in range(2, PACK):
             gather0(j)
             gather1(j)

@@ -24,6 +24,7 @@ BLOCKS = N // P
 LIST = 16
 HALF = V // 2
 CUTS = [(0, 256), (256, 512)]
+SHARE = 320
 
 
 def tile_picked_spconv_relu_e_kernel(tc, xT, w1, w2, offs, to1, to2, out):
@@ -149,8 +150,10 @@ def tile_picked_spconv_relu_e_kernel(tc, xT, w1, w2, offs, to1, to2, out):
         y01 = leave(nc.scalar.copy, "y01", second[0][:])
         scatter_s(0, 1, y01[:])
         scatter_v(1, 1, y11[:])
-        finish(0, 0, 256, nc.gpsimd, relu_s)
-        finish(0, 256, U, nc.gpsimd, relu_s)
+        finish(0, 0, SHARE, nc.gpsimd, relu_s)
+        total = keep.tile([P, V], F32, name="total0", tag="y01", align_bytes=64)
+        nc.vector.tensor_tensor(total[:, 0:U - SHARE], cells[0][0][:, SHARE:U], cells[1][0][:, SHARE:U], ADD)
+        store(0, SHARE, U, total[:, 0:U - SHARE], relu_s)
         totals = [add(1, lo, hi, nc.vector) for lo, hi in CUTS]
         for h, relu in enumerate([relu_v, relu_v]):
             store(1, CUTS[h][0], CUTS[h][1], totals[h], relu)

@@ -12,8 +12,6 @@ U16 = mybir.dt.uint16
 U8 = mybir.dt.uint8
 FP8X4 = mybir.dt.float8_e4m3fn_x4
 ADD = mybir.AluOpType.add
-MULT = mybir.AluOpType.mult
-MAX = mybir.AluOpType.max
 RELU = mybir.ActivationFunctionType.Relu
 COPY = mybir.ActivationFunctionType.Copy
 
@@ -25,6 +23,7 @@ LIST = 16
 HALF = V // 2
 CUTS = [(0, 256), (256, 512)]
 SHARE = 320
+HEAD = 192
 
 
 def tile_picked_spconv_relu_e_kernel(tc, xT, w1, w2, offs, to1, to2, out):
@@ -36,7 +35,7 @@ def tile_picked_spconv_relu_e_kernel(tc, xT, w1, w2, offs, to1, to2, out):
         offs_sb = keep.tile([P, S // LIST], U16, name="offs_sb")
         to_sb = [keep.tile([P, V // LIST], U16, name="to_sb%d" % d) for d in range(TAPS)]
         x_rows = xT.rearrange("(p j) t -> p j t", j=PACK)
-        x_sb = [keep.tile([P, T], F32, name="x_sb%d" % j) for j in range(PACK)]
+        x_sb = [keep.tile([P, T], F32, name="x_sb%d" % j, tag="x_sb%d" % j, align_bytes=64) for j in range(PACK)]
         w_rows = [w.rearrange("(p j) n -> p j n", j=PACK) for w in (w1, w2)]
         w_sb = [[keep.tile([P, PACK, P], F32, name="w_sb%d_%d" % (d, b), tag="w_sb%d_%d" % (d, b), align_bytes=64) for b in range(BLOCKS)] for d in range(TAPS)]
 
@@ -51,7 +50,7 @@ def tile_picked_spconv_relu_e_kernel(tc, xT, w1, w2, offs, to1, to2, out):
         nc.sync.dma_start(to_sb[0][:], to1)
         nc.sync.dma_start(to_sb[1][:], to2)
 
-        cells = [[keep.tile([P, U], F32, name="cells%d_%d" % (d, b)) for b in range(BLOCKS)] for d in range(TAPS)]
+        cells = [[keep.tile([P, U], F32, name="cells%d_%d" % (d, b), tag="cells%d_%d" % (d, b)) for b in range(BLOCKS)] for d in range(TAPS)]
         for b in range(BLOCKS):
             nc.vector.memset(cells[1][b][:], 0.0)
             nc.scalar.copy(cells[0][b][:], cells[1][b][:])
@@ -79,7 +78,7 @@ def tile_picked_spconv_relu_e_kernel(tc, xT, w1, w2, offs, to1, to2, out):
             return codes[:], scales[:]
 
         first = [psum.tile([P, V], F32, name="first%d" % d) for d in range(TAPS)]
-        second = [psum.tile([P, V], F32, name="second%d" % d) for d in range(TAPS)]
+        second = psum.tile([P, TAPS, V], F32, name="second")
 
         def multiply(acc, xq, wq):
             nc.tensor.matmul_mx(out=acc, lhsT=wq[0].bitcast(FP8X4), lhsT_scale=wq[1],
@@ -102,21 +101,16 @@ def tile_picked_spconv_relu_e_kernel(tc, xT, w1, w2, offs, to1, to2, out):
         def relu_v(res, total):
             nc.vector.tensor_scalar_max(res, total, 0.0)
 
-        def relu_g(res, total):
-            nc.gpsimd.tensor_scalar(res, total, 1.0, 0.0, MULT, MAX)
-
-        def add(b, lo, hi, adder):
-            total = keep.tile([P, hi - lo], F32, name="total%d_%d" % (b, lo))
+        def add(b, lo, hi, adder, tag=None):
+            name = "total%d_%d" % (b, lo)
+            total = keep.tile([P, hi - lo], F32, name=name, tag=tag or name)
             adder.tensor_tensor(total[:], cells[0][b][:, lo:hi], cells[1][b][:, lo:hi], ADD)
             return total
 
-        def store(b, lo, hi, total, relu):
+        def store(b, lo, hi, total, relu, queue):
             res = keep.tile([P, hi - lo], F32, name="res%d_%d" % (b, lo))
             relu(res[:], total[:])
-            [nc.scalar, nc.sync][b].dma_start(out[b * P:(b + 1) * P, lo:hi], res[:])
-
-        def finish(b, lo, hi, adder, relu):
-            store(b, lo, hi, add(b, lo, hi, adder), relu)
+            queue.dma_start(out[b * P:(b + 1) * P, lo:hi], res[:])
 
         def weave_w(copy, d, b):
             woven = keep.tile([P, P, PACK], BF16, name="w_woven%d_%d" % (d, b), tag="w_woven%d_%d" % (d, b), align_bytes=64)
@@ -132,28 +126,31 @@ def tile_picked_spconv_relu_e_kernel(tc, xT, w1, w2, offs, to1, to2, out):
             gather0(j)
             gather1(j)
         weave(nc.vector.tensor_copy, x_woven[1][:, :, 2:4], pairs[1][:])
-        xq0 = quantize("x0", x_woven[0][:], V)
+        xq0 = quantize("x0", x_woven[0][:], V, "x_sb3")
         ww = [[None, None], [None, None]]
-        for b in range(BLOCKS):
-            for d in range(TAPS):
-                ww[d][b] = weave_w(nc.scalar.copy, d, b)
+        ww[0][0] = weave_w(nc.scalar.copy, 0, 0)
+        ww[1][0] = weave_w(nc.scalar.copy, 1, 0)
+        ww[0][1] = weave_w(nc.scalar.copy, 0, 1)
         multiply(first[0][:], xq0, quantize("w00", ww[0][0], P))
         xq1 = quantize("x1", x_woven[1][:], V, "w_sb0_0")
         multiply(first[1][:], xq1, quantize("w10", ww[1][0], P))
-        y00 = leave(nc.vector.tensor_copy, "y00", first[0][:], "w_woven1_0")
-        multiply(second[0][:], xq0, quantize("w01", ww[0][1], P))
-        y10 = leave(nc.vector.tensor_copy, "y10", first[1][:])
-        multiply(second[1][:], xq1, quantize("w11", ww[1][1], P))
-        scatter_s(0, 0, y00[:])
+        ww[1][1] = weave_w(nc.vector.tensor_copy, 1, 1)
+        multiply(second[:, 0, :], xq0, quantize("w01", ww[0][1], P))
+        multiply(second[:, 1, :], xq1, quantize("w11", ww[1][1], P))
+        y00a = leave(nc.scalar.copy, "y00a", first[0][:, 0:HEAD])
+        y10 = leave(nc.vector.tensor_copy, "y10", first[1][:], "w_sb0_1")
+        nc.scalar.activation(cells[0][0][:].indirect(entries(to_sb[0], 0, HEAD)), y00a[:], COPY)
         scatter_v(1, 0, y10[:])
-        y11 = leave(nc.scalar.copy, "y11", second[1][:])
-        y01 = leave(nc.scalar.copy, "y01", second[0][:])
+        y00b = leave(nc.scalar.copy, "y00b", first[0][:, HEAD:V], "w11")
+        y11 = leave(nc.scalar.copy, "y11", second[:, 1, :])
+        y01 = leave(nc.scalar.copy, "y01", second[:, 0, :])
+        nc.scalar.activation(cells[0][0][:].indirect(entries(to_sb[0], HEAD, V)), y00b[:], COPY)
         scatter_s(0, 1, y01[:])
         scatter_v(1, 1, y11[:])
-        finish(0, 0, SHARE, nc.gpsimd, relu_s)
-        total = keep.tile([P, V], F32, name="total0", tag="y01", align_bytes=64)
+        store(0, 0, SHARE, add(0, 0, SHARE, nc.gpsimd), relu_v, nc.sync)
+        total = keep.tile([P, V], F32, name="total0")
         nc.vector.tensor_tensor(total[:, 0:U - SHARE], cells[0][0][:, SHARE:U], cells[1][0][:, SHARE:U], ADD)
-        store(0, SHARE, U, total[:, 0:U - SHARE], relu_s)
-        totals = [add(1, lo, hi, nc.vector) for lo, hi in CUTS]
+        store(0, SHARE, U, total[:, 0:U - SHARE], relu_s, nc.scalar)
+        totals = [add(1, lo, hi, nc.vector, "cells%d_0" % h) for h, (lo, hi) in enumerate(CUTS)]
         for h, relu in enumerate([relu_v, relu_v]):
-            store(1, CUTS[h][0], CUTS[h][1], totals[h], relu)
+            store(1, CUTS[h][0], CUTS[h][1], totals[h], relu, nc.sync)

@@ -22,7 +22,6 @@ BLOCKS = N // P
 LIST = 16
 HALF = V // 2
 CUTS = [(0, 256), (256, 512)]
-SHARE = 320
 HEAD = 192
 
 
@@ -147,10 +146,9 @@ def tile_picked_spconv_relu_e_kernel(tc, xT, w1, w2, offs, to1, to2, out):
         nc.scalar.activation(cells[0][0][:].indirect(entries(to_sb[0], HEAD, V)), y00b[:], COPY)
         scatter_s(0, 1, y01[:])
         scatter_v(1, 1, y11[:])
-        store(0, 0, SHARE, add(0, 0, SHARE, nc.gpsimd), relu_v, nc.sync)
-        total = keep.tile([P, V], F32, name="total0")
-        nc.vector.tensor_tensor(total[:, 0:U - SHARE], cells[0][0][:, SHARE:U], cells[1][0][:, SHARE:U], ADD)
-        store(0, SHARE, U, total[:, 0:U - SHARE], relu_s, nc.scalar)
+        finish0 = [add(0, lo, hi, nc.gpsimd) for lo, hi in CUTS]
+        store(0, CUTS[0][0], CUTS[0][1], finish0[0], relu_v, nc.sync)
+        store(0, CUTS[1][0], CUTS[1][1], finish0[1], relu_s, nc.scalar)
         totals = [add(1, lo, hi, nc.vector, "cells%d_0" % h) for h, (lo, hi) in enumerate(CUTS)]
         for h, relu in enumerate([relu_v, relu_v]):
             store(1, CUTS[h][0], CUTS[h][1], totals[h], relu, nc.sync)

@@ -23,6 +23,7 @@ LIST = 16
 HALF = V // 2
 CUTS = [(0, 256), (256, 512)]
 HEAD = 192
+SHARE = 384
 
 
 def tile_picked_spconv_relu_e_kernel(tc, xT, w1, w2, offs, to1, to2, out):
@@ -77,7 +78,7 @@ def tile_picked_spconv_relu_e_kernel(tc, xT, w1, w2, offs, to1, to2, out):
             return codes[:], scales[:]
 
         first = [psum.tile([P, V], F32, name="first%d" % d) for d in range(TAPS)]
-        second = psum.tile([P, TAPS, V], F32, name="second")
+        second = [psum.tile([P, V], F32, name="second%d" % d) for d in range(TAPS)]
 
         def multiply(acc, xq, wq):
             nc.tensor.matmul_mx(out=acc, lhsT=wq[0].bitcast(FP8X4), lhsT_scale=wq[1],
@@ -100,15 +101,9 @@ def tile_picked_spconv_relu_e_kernel(tc, xT, w1, w2, offs, to1, to2, out):
         def relu_v(res, total):
             nc.vector.tensor_scalar_max(res, total, 0.0)
 
-        def add(b, lo, hi, adder, tag=None):
-            name = "total%d_%d" % (b, lo)
-            total = keep.tile([P, hi - lo], F32, name=name, tag=tag or name)
-            adder.tensor_tensor(total[:], cells[0][b][:, lo:hi], cells[1][b][:, lo:hi], ADD)
-            return total
-
         def store(b, lo, hi, total, relu, queue):
             res = keep.tile([P, hi - lo], F32, name="res%d_%d" % (b, lo))
-            relu(res[:], total[:])
+            relu(res[:], total)
             queue.dma_start(out[b * P:(b + 1) * P, lo:hi], res[:])
 
         def weave_w(copy, d, b):
@@ -134,21 +129,25 @@ def tile_picked_spconv_relu_e_kernel(tc, xT, w1, w2, offs, to1, to2, out):
         xq1 = quantize("x1", x_woven[1][:], V, "w_sb0_0")
         multiply(first[1][:], xq1, quantize("w10", ww[1][0], P))
         ww[1][1] = weave_w(nc.vector.tensor_copy, 1, 1)
-        multiply(second[:, 0, :], xq0, quantize("w01", ww[0][1], P))
-        multiply(second[:, 1, :], xq1, quantize("w11", ww[1][1], P))
+        multiply(second[0][:], xq0, quantize("w01", ww[0][1], P))
+        multiply(second[1][:], xq1, quantize("w11", ww[1][1], P))
         y00a = leave(nc.scalar.copy, "y00a", first[0][:, 0:HEAD])
         y10 = leave(nc.vector.tensor_copy, "y10", first[1][:], "w_sb0_1")
         nc.scalar.activation(cells[0][0][:].indirect(entries(to_sb[0], 0, HEAD)), y00a[:], COPY)
         scatter_v(1, 0, y10[:])
-        y00b = leave(nc.scalar.copy, "y00b", first[0][:, HEAD:V], "w11")
-        y11 = leave(nc.scalar.copy, "y11", second[:, 1, :])
-        y01 = leave(nc.scalar.copy, "y01", second[:, 0, :])
+        y01 = leave(nc.scalar.copy, "y01", second[0][:])
+        y00b = leave(nc.scalar.copy, "y00b", first[0][:, HEAD:V], "w01")
+        y11 = leave(nc.scalar.copy, "y11", second[1][:])
         nc.scalar.activation(cells[0][0][:].indirect(entries(to_sb[0], HEAD, V)), y00b[:], COPY)
         scatter_s(0, 1, y01[:])
         scatter_v(1, 1, y11[:])
-        finish0 = [add(0, lo, hi, nc.gpsimd) for lo, hi in CUTS]
-        store(0, CUTS[0][0], CUTS[0][1], finish0[0], relu_v, nc.sync)
-        store(0, CUTS[1][0], CUTS[1][1], finish0[1], relu_s, nc.scalar)
-        totals = [add(1, lo, hi, nc.vector, "cells%d_0" % h) for h, (lo, hi) in enumerate(CUTS)]
+        total0 = keep.tile([P, U], F32, name="total0")
+        for adder, lo, hi in [(nc.gpsimd, 0, V), (nc.gpsimd, V, SHARE), (nc.vector, SHARE, U)]:
+            adder.tensor_tensor(total0[:, lo:hi], cells[0][0][:, lo:hi], cells[1][0][:, lo:hi], ADD)
+        store(0, 0, V, total0[:, 0:V], relu_v, nc.sync)
+        store(0, V, U, total0[:, V:U], relu_s, nc.scalar)
+        totals = [cells[d][0][:, 0:V] for d in range(TAPS)]
+        for h, (lo, hi) in enumerate(CUTS):
+            nc.vector.tensor_tensor(totals[h], cells[0][1][:, lo:hi], cells[1][1][:, lo:hi], ADD)
         for h, relu in enumerate([relu_v, relu_v]):
             store(1, CUTS[h][0], CUTS[h][1], totals[h], relu, nc.sync)

@@ -23,7 +23,6 @@ LIST = 16
 HALF = V // 2
 CUTS = [(0, 256), (256, 512)]
 HEAD = 192
-SHARE = 384
 
 
 def tile_picked_spconv_relu_e_kernel(tc, xT, w1, w2, offs, to1, to2, out):
@@ -142,11 +141,11 @@ def tile_picked_spconv_relu_e_kernel(tc, xT, w1, w2, offs, to1, to2, out):
         scatter_s(0, 1, y01[:])
         scatter_v(1, 1, y11[:])
         total0 = keep.tile([P, U], F32, name="total0")
-        for adder, lo, hi in [(nc.gpsimd, 0, V), (nc.gpsimd, V, SHARE), (nc.vector, SHARE, U)]:
+        for adder, lo, hi in [(nc.vector, 0, V), (nc.vector, V, U)]:
             adder.tensor_tensor(total0[:, lo:hi], cells[0][0][:, lo:hi], cells[1][0][:, lo:hi], ADD)
-        store(0, 0, V, total0[:, 0:V], relu_v, nc.sync)
+        store(0, 0, V, total0[:, 0:V], relu_s, nc.scalar)
         store(0, V, U, total0[:, V:U], relu_s, nc.scalar)
-        totals = [cells[d][0][:, 0:V] for d in range(TAPS)]
+        totals = [keep.tile([P, V], F32, name="total1_%d" % h)[:] for h in range(2)]
         for h, (lo, hi) in enumerate(CUTS):
             nc.vector.tensor_tensor(totals[h], cells[0][1][:, lo:hi], cells[1][1][:, lo:hi], ADD)
         for h, relu in enumerate([relu_v, relu_v]):

@@ -140,12 +140,12 @@ def tile_picked_spconv_relu_e_kernel(tc, xT, w1, w2, offs, to1, to2, out):
         nc.scalar.activation(cells[0][0][:].indirect(entries(to_sb[0], HEAD, V)), y00b[:], COPY)
         scatter_s(0, 1, y01[:])
         scatter_v(1, 1, y11[:])
-        total0 = keep.tile([P, U], F32, name="total0")
-        for adder, lo, hi in [(nc.vector, 0, V), (nc.vector, V, U)]:
-            adder.tensor_tensor(total0[:, lo:hi], cells[0][0][:, lo:hi], cells[1][0][:, lo:hi], ADD)
-        store(0, 0, V, total0[:, 0:V], relu_s, nc.scalar)
-        store(0, V, U, total0[:, V:U], relu_s, nc.scalar)
-        totals = [keep.tile([P, V], F32, name="total1_%d" % h)[:] for h in range(2)]
+        total0 = keep.tile([P, V], F32, name="total0")
+        nc.gpsimd.tensor_tensor(total0[:], cells[0][0][:, 0:V], cells[1][0][:, 0:V], ADD)
+        nc.vector.tensor_tensor(cells[0][0][:, 0:V], cells[0][0][:, V:U], cells[1][0][:, V:U], ADD)
+        store(0, 0, V, total0[:], relu_s, nc.sync)
+        store(0, V, U, cells[0][0][:, 0:V], relu_s, nc.scalar)
+        totals = [cells[1][0][:, lo:hi] for lo, hi in CUTS]
         for h, (lo, hi) in enumerate(CUTS):
             nc.vector.tensor_tensor(totals[h], cells[0][1][:, lo:hi], cells[1][1][:, lo:hi], ADD)
         for h, relu in enumerate([relu_v, relu_v]):

@@ -34,7 +34,7 @@ def tile_picked_spconv_relu_e_kernel(tc, xT, w1, w2, offs, to1, to2, out):
         offs_sb = keep.tile([P, S // LIST], U16, name="offs_sb")
         to_sb = [keep.tile([P, V // LIST], U16, name="to_sb%d" % d) for d in range(TAPS)]
         x_rows = xT.rearrange("(p j) t -> p j t", j=PACK)
-        x_sb = [keep.tile([P, T], F32, name="x_sb%d" % j, tag="x_sb%d" % j, align_bytes=64) for j in range(PACK)]
+        x_sb = [keep.tile([P, T], F32, name="x_sb%d" % j) for j in range(PACK)]
         w_rows = [w.rearrange("(p j) n -> p j n", j=PACK) for w in (w1, w2)]
         w_sb = [[keep.tile([P, PACK, P], F32, name="w_sb%d_%d" % (d, b), tag="w_sb%d_%d" % (d, b), align_bytes=64) for b in range(BLOCKS)] for d in range(TAPS)]
 
@@ -119,7 +119,7 @@ def tile_picked_spconv_relu_e_kernel(tc, xT, w1, w2, offs, to1, to2, out):
             gather0(j)
             gather1(j)
         weave(nc.vector.tensor_copy, x_woven[1][:, :, 2:4], pairs[1][:])
-        xq0 = quantize("x0", x_woven[0][:], V, "x_sb3")
+        xq0 = quantize("x0", x_woven[0][:], V)
         ww = [[None, None], [None, None]]
         ww[0][0] = weave_w(nc.scalar.copy, 0, 0)
         ww[1][0] = weave_w(nc.scalar.copy, 1, 0)
@@ -143,7 +143,7 @@ def tile_picked_spconv_relu_e_kernel(tc, xT, w1, w2, offs, to1, to2, out):
         total0 = keep.tile([P, V], F32, name="total0")
         nc.gpsimd.tensor_tensor(total0[:], cells[0][0][:, 0:V], cells[1][0][:, 0:V], ADD)
         nc.vector.tensor_tensor(cells[0][0][:, 0:V], cells[0][0][:, V:U], cells[1][0][:, V:U], ADD)
-        store(0, 0, V, total0[:], relu_s, nc.sync)
+        store(0, 0, V, total0[:], relu_s, nc.scalar)
         store(0, V, U, cells[0][0][:, 0:V], relu_s, nc.scalar)
         totals = [cells[1][0][:, lo:hi] for lo, hi in CUTS]
         for h, (lo, hi) in enumerate(CUTS):

@@ -34,7 +34,7 @@ def tile_picked_spconv_relu_e_kernel(tc, xT, w1, w2, offs, to1, to2, out):
         offs_sb = keep.tile([P, S // LIST], U16, name="offs_sb")
         to_sb = [keep.tile([P, V // LIST], U16, name="to_sb%d" % d) for d in range(TAPS)]
         x_rows = xT.rearrange("(p j) t -> p j t", j=PACK)
-        x_sb = [keep.tile([P, T], F32, name="x_sb%d" % j) for j in range(PACK)]
+        x_sb = [keep.tile([P, T], F32, name="x_sb%d" % j, tag="x_last" if j == PACK - 1 else "x_sb%d" % j, align_bytes=64) for j in range(PACK)]
         w_rows = [w.rearrange("(p j) n -> p j n", j=PACK) for w in (w1, w2)]
         w_sb = [[keep.tile([P, PACK, P], F32, name="w_sb%d_%d" % (d, b), tag="w_sb%d_%d" % (d, b), align_bytes=64) for b in range(BLOCKS)] for d in range(TAPS)]
 
@@ -76,8 +76,7 @@ def tile_picked_spconv_relu_e_kernel(tc, xT, w1, w2, offs, to1, to2, out):
                                   in_=woven.rearrange("p w j -> p (w j)"))
             return codes[:], scales[:]
 
-        first = [psum.tile([P, V], F32, name="first%d" % d) for d in range(TAPS)]
-        second = [psum.tile([P, V], F32, name="second%d" % d) for d in range(TAPS)]
+        first1 = [psum.tile([P, HALF], F32, name="first1_%d" % h) for h in range(2)]
 
         def multiply(acc, xq, wq):
             nc.tensor.matmul_mx(out=acc, lhsT=wq[0].bitcast(FP8X4), lhsT_scale=wq[1],
@@ -119,26 +118,47 @@ def tile_picked_spconv_relu_e_kernel(tc, xT, w1, w2, offs, to1, to2, out):
             gather0(j)
             gather1(j)
         weave(nc.vector.tensor_copy, x_woven[1][:, :, 2:4], pairs[1][:])
-        xq0 = quantize("x0", x_woven[0][:], V)
+        xq0 = quantize("x0", x_woven[0][:], V, "x_last")
         ww = [[None, None], [None, None]]
         ww[0][0] = weave_w(nc.scalar.copy, 0, 0)
         ww[1][0] = weave_w(nc.scalar.copy, 1, 0)
-        ww[0][1] = weave_w(nc.scalar.copy, 0, 1)
-        multiply(first[0][:], xq0, quantize("w00", ww[0][0], P))
+        shared = keep.tile([P, P, PACK], BF16, name="w_woven0_1", align_bytes=64)
+        ww[0][1] = shared[:]
+        weave(nc.scalar.copy, shared[:, 0:P // 2, :], w_sb[0][1][:, :, 0:P // 2])
+        wq00 = quantize("w00", ww[0][0], P)
+        half0 = psum.tile([P, HALF], F32, name="half0")
+        late = psum.tile([P, U], F32, name="late")
+        halves = [half0[:], late[:, 0:HALF]]
+        for h in range(2):
+            cols = slice(h * HALF, (h + 1) * HALF)
+            multiply(halves[h], (xq0[0][:, cols], xq0[1][:, cols]), wq00)
         xq1 = quantize("x1", x_woven[1][:], V, "w_sb0_0")
-        multiply(first[1][:], xq1, quantize("w10", ww[1][0], P))
+        weave(nc.vector.tensor_copy, shared[:, P // 2:P, :], w_sb[0][1][:, :, P // 2:P])
+        wq10 = quantize("w10", ww[1][0], P)
+        for h in range(2):
+            cols = slice(h * HALF, (h + 1) * HALF)
+            multiply(first1[h][:], (xq1[0][:, cols], xq1[1][:, cols]), wq10)
+        wq01 = quantize("w01", ww[0][1], P)
+        y00a = keep.tile([P, HEAD], F32, name="y00a", align_bytes=64)
+        nc.scalar.copy(y00a[:, 0:HALF], halves[0])
+        nc.scalar.copy(y00a[:, HALF:HEAD], halves[1][:, 0:HEAD - HALF])
+        early = psum.tile([P, HALF], F32, name="early")
+        multiply(early[:], (xq0[0][:, HALF:V], xq0[1][:, HALF:V]), wq01)
+        multiply(late[:, HALF:V], (xq0[0][:, 0:HALF], xq0[1][:, 0:HALF]), wq01)
         ww[1][1] = weave_w(nc.vector.tensor_copy, 1, 1)
-        multiply(second[0][:], xq0, quantize("w01", ww[0][1], P))
-        multiply(second[1][:], xq1, quantize("w11", ww[1][1], P))
-        y00a = leave(nc.scalar.copy, "y00a", first[0][:, 0:HEAD])
-        y10 = leave(nc.vector.tensor_copy, "y10", first[1][:], "w_sb0_1")
+        y10 = keep.tile([P, V], F32, name="y10", tag="w_sb0_1", align_bytes=64)
+        for h in range(2):
+            nc.vector.tensor_copy(y10[:, h * HALF:(h + 1) * HALF], first1[h][:])
+        multiply(late[:, V:U], xq1, quantize("w11", ww[1][1], P, "w10"))
         nc.scalar.activation(cells[0][0][:].indirect(entries(to_sb[0], 0, HEAD)), y00a[:], COPY)
         scatter_v(1, 0, y10[:])
-        y01 = leave(nc.scalar.copy, "y01", second[0][:])
-        y00b = leave(nc.scalar.copy, "y00b", first[0][:, HEAD:V], "w01")
-        y11 = leave(nc.scalar.copy, "y11", second[1][:])
-        nc.scalar.activation(cells[0][0][:].indirect(entries(to_sb[0], HEAD, V)), y00b[:], COPY)
-        scatter_s(0, 1, y01[:])
+        rest = V - HEAD
+        y0 = keep.tile([P, rest + V], F32, name="y0", align_bytes=64)
+        nc.scalar.copy(y0[:, rest + HALF:rest + V], early[:])
+        nc.scalar.copy(y0[:, 0:rest + HALF], late[:, HALF - rest:V])
+        y11 = leave(nc.scalar.copy, "y11", late[:, V:U])
+        nc.scalar.activation(cells[0][0][:].indirect(entries(to_sb[0], HEAD, V)), y0[:, 0:rest], COPY)
+        scatter_s(0, 1, y0[:, rest:rest + V])
         scatter_v(1, 1, y11[:])
         total0 = keep.tile([P, V], F32, name="total0")
         nc.gpsimd.tensor_tensor(total0[:], cells[0][0][:, 0:V], cells[1][0][:, 0:V], ADD)

@@ -124,7 +124,7 @@ def tile_picked_spconv_relu_e_kernel(tc, xT, w1, w2, offs, to1, to2, out):
         ww[1][0] = weave_w(nc.scalar.copy, 1, 0)
         shared = keep.tile([P, P, PACK], BF16, name="w_woven0_1", align_bytes=64)
         ww[0][1] = shared[:]
-        weave(nc.scalar.copy, shared[:, 0:P // 2, :], w_sb[0][1][:, :, 0:P // 2])
+        weave(nc.scalar.copy, shared[:], w_sb[0][1][:])
         wq00 = quantize("w00", ww[0][0], P)
         half0 = psum.tile([P, HALF], F32, name="half0")
         late = psum.tile([P, U], F32, name="late")
@@ -133,19 +133,18 @@ def tile_picked_spconv_relu_e_kernel(tc, xT, w1, w2, offs, to1, to2, out):
             cols = slice(h * HALF, (h + 1) * HALF)
             multiply(halves[h], (xq0[0][:, cols], xq0[1][:, cols]), wq00)
         xq1 = quantize("x1", x_woven[1][:], V, "w_sb0_0")
-        weave(nc.vector.tensor_copy, shared[:, P // 2:P, :], w_sb[0][1][:, :, P // 2:P])
         wq10 = quantize("w10", ww[1][0], P)
         for h in range(2):
             cols = slice(h * HALF, (h + 1) * HALF)
             multiply(first1[h][:], (xq1[0][:, cols], xq1[1][:, cols]), wq10)
+        ww[1][1] = weave_w(nc.vector.tensor_copy, 1, 1)
         wq01 = quantize("w01", ww[0][1], P)
-        y00a = keep.tile([P, HEAD], F32, name="y00a", align_bytes=64)
+        y00a = keep.tile([P, HEAD], F32, name="y00a", tag="w_woven1_0", align_bytes=64)
         nc.scalar.copy(y00a[:, 0:HALF], halves[0])
         nc.scalar.copy(y00a[:, HALF:HEAD], halves[1][:, 0:HEAD - HALF])
         early = psum.tile([P, HALF], F32, name="early")
         multiply(early[:], (xq0[0][:, HALF:V], xq0[1][:, HALF:V]), wq01)
         multiply(late[:, HALF:V], (xq0[0][:, 0:HALF], xq0[1][:, 0:HALF]), wq01)
-        ww[1][1] = weave_w(nc.vector.tensor_copy, 1, 1)
         y10 = keep.tile([P, V], F32, name="y10", tag="w_sb0_1", align_bytes=64)
         for h in range(2):
             nc.vector.tensor_copy(y10[:, h * HALF:(h + 1) * HALF], first1[h][:])

@@ -23,6 +23,7 @@ LIST = 16
 HALF = V // 2
 CUTS = [(0, 256), (256, 512)]
 HEAD = 192
+SHARE = 64
 
 
 def tile_picked_spconv_relu_e_kernel(tc, xT, w1, w2, offs, to1, to2, out):
@@ -137,11 +138,14 @@ def tile_picked_spconv_relu_e_kernel(tc, xT, w1, w2, offs, to1, to2, out):
         for h in range(2):
             cols = slice(h * HALF, (h + 1) * HALF)
             multiply(first1[h][:], (xq1[0][:, cols], xq1[1][:, cols]), wq10)
-        ww[1][1] = weave_w(nc.vector.tensor_copy, 1, 1)
+        last = keep.tile([P, P, PACK], BF16, name="w_woven1_1", align_bytes=64)
+        ww[1][1] = last[:]
+        weave(nc.vector.tensor_copy, last[:, 0:SHARE, :], w_sb[1][1][:, :, 0:SHARE])
         wq01 = quantize("w01", ww[0][1], P)
         y00a = keep.tile([P, HEAD], F32, name="y00a", tag="w_woven1_0", align_bytes=64)
         nc.scalar.copy(y00a[:, 0:HALF], halves[0])
         nc.scalar.copy(y00a[:, HALF:HEAD], halves[1][:, 0:HEAD - HALF])
+        weave(nc.scalar.copy, last[:, SHARE:P, :], w_sb[1][1][:, :, SHARE:P])
         early = psum.tile([P, HALF], F32, name="early")
         multiply(early[:], (xq0[0][:, HALF:V], xq0[1][:, HALF:V]), wq01)
         multiply(late[:, HALF:V], (xq0[0][:, 0:HALF], xq0[1][:, 0:HALF]), wq01)

from contextlib import ExitStack

import concourse.mybir as mybir

K, T, S, V, N, U = 512, 1024, 512, 256, 256, 512
FLOPS = 2 * K * N * S

F32 = mybir.dt.float32
BF16 = mybir.dt.bfloat16
U32 = mybir.dt.uint32
U16 = mybir.dt.uint16
U8 = mybir.dt.uint8
FP8X4 = mybir.dt.float8_e4m3fn_x4
ADD = mybir.AluOpType.add
RELU = mybir.ActivationFunctionType.Relu
COPY = mybir.ActivationFunctionType.Copy

P = 128
PACK = 4
TAPS = 2
BLOCKS = N // P
LIST = 16
HALF = V // 2
CUTS = [(0, 256), (256, 512)]
HEAD = 192
SHARE = 64


def tile_picked_spconv_relu_e_kernel(tc, xT, w1, w2, offs, to1, to2, out):
    nc = tc.nc
    with ExitStack() as ctx:
        keep = ctx.enter_context(tc.tile_pool(name="keep", bufs=1))
        psum = ctx.enter_context(tc.psum_pool(name="psum", bufs=1))

        offs_sb = keep.tile([P, S // LIST], U16, name="offs_sb")
        to_sb = [keep.tile([P, V // LIST], U16, name="to_sb%d" % d) for d in range(TAPS)]
        x_rows = xT.rearrange("(p j) t -> p j t", j=PACK)
        x_sb = [keep.tile([P, T], F32, name="x_sb%d" % j, tag="x_last" if j == PACK - 1 else "x_sb%d" % j, align_bytes=64) for j in range(PACK)]
        w_rows = [w.rearrange("(p j) n -> p j n", j=PACK) for w in (w1, w2)]
        w_sb = [[keep.tile([P, PACK, P], F32, name="w_sb%d_%d" % (d, b), tag="w_sb%d_%d" % (d, b), align_bytes=64) for b in range(BLOCKS)] for d in range(TAPS)]

        nc.sync.dma_start(x_sb[0][:], x_rows[:, 0, :])
        nc.sync.dma_start(offs_sb[:], offs)
        nc.sync.dma_start(x_sb[1][:], x_rows[:, 1, :])
        nc.sync.dma_start(x_sb[2][:], x_rows[:, 2, :])
        nc.sync.dma_start(x_sb[3][:], x_rows[:, 3, :])
        for b in range(BLOCKS):
            for d in range(TAPS):
                nc.sync.dma_start(w_sb[d][b][:], w_rows[d][:, :, b * P:(b + 1) * P])
        nc.sync.dma_start(to_sb[0][:], to1)
        nc.sync.dma_start(to_sb[1][:], to2)

        cells = [[keep.tile([P, U], F32, name="cells%d_%d" % (d, b), tag="cells%d_%d" % (d, b)) for b in range(BLOCKS)] for d in range(TAPS)]
        for b in range(BLOCKS):
            nc.vector.memset(cells[1][b][:], 0.0)
            nc.scalar.copy(cells[0][b][:], cells[1][b][:])

        def entries(lists, lo, hi):
            return lists[:, lo // LIST:hi // LIST]

        x_woven = [keep.tile([P, V, PACK], BF16, name="x_woven%d" % d, align_bytes=64) for d in range(TAPS)]
        pairs = [keep.tile([P, 2, V], BF16, name="pairs%d" % h) for h in range(2)]

        def gather0(j):
            nc.vector.tensor_copy(x_woven[0][:, :, j], x_sb[j][:].indirect(entries(offs_sb, 0, V)))

        def gather1(j):
            nc.scalar.activation(pairs[j // 2][:, j % 2, :], x_sb[j][:].indirect(entries(offs_sb, V, S)), COPY)

        def weave(copy, woven, planes):
            copy(woven.rearrange("p (c i) j -> p c j i", i=2), planes.rearrange("p j (c i) -> p c j i", i=2))

        def quantize(name, woven, width, tag=None):
            codes = keep.tile([P, width], U32, name=name + "_codes", tag=tag or name, align_bytes=64)
            scales = keep.tile([P, width], U8, name=name + "_scales", align_bytes=64)
            nc.vector.quantize_mx(out=codes[:].bitcast(FP8X4), scales=scales[:],
                                  in_=woven.rearrange("p w j -> p (w j)"))
            return codes[:], scales[:]

        first1 = [psum.tile([P, HALF], F32, name="first1_%d" % h) for h in range(2)]

        def multiply(acc, xq, wq):
            nc.tensor.matmul_mx(out=acc, lhsT=wq[0].bitcast(FP8X4), lhsT_scale=wq[1],
                                rhs=xq[0].bitcast(FP8X4), rhs_scale=xq[1], start=True, stop=True)

        def leave(copy, name, acc, tag=None):
            y = keep.tile([P, acc.shape[1]], F32, name=name, tag=tag or name, align_bytes=64)
            copy(y[:], acc)
            return y

        def scatter_v(d, b, y):
            nc.vector.tensor_copy(cells[d][b][:].indirect(to_sb[d][:]), y)

        def scatter_s(d, b, y):
            nc.scalar.activation(cells[d][b][:].indirect(to_sb[d][:]), y, COPY)

        def relu_s(res, total):
            nc.scalar.activation(res, total, RELU)

        def relu_v(res, total):
            nc.vector.tensor_scalar_max(res, total, 0.0)

        def store(b, lo, hi, total, relu, queue):
            res = keep.tile([P, hi - lo], F32, name="res%d_%d" % (b, lo))
            relu(res[:], total)
            queue.dma_start(out[b * P:(b + 1) * P, lo:hi], res[:])

        def weave_w(copy, d, b):
            woven = keep.tile([P, P, PACK], BF16, name="w_woven%d_%d" % (d, b), tag="w_woven%d_%d" % (d, b), align_bytes=64)
            weave(copy, woven[:], w_sb[d][b][:])
            return woven[:]

        for j in range(2):
            gather0(j)
            gather1(j)
        weave(nc.vector.tensor_copy, x_woven[1][:, 0:HALF, 0:2], pairs[0][:, :, 0:HALF])
        weave(nc.scalar.copy, x_woven[1][:, HALF:V, 0:2], pairs[0][:, :, HALF:V])
        for j in range(2, PACK):
            gather0(j)
            gather1(j)
        weave(nc.vector.tensor_copy, x_woven[1][:, :, 2:4], pairs[1][:])
        xq0 = quantize("x0", x_woven[0][:], V, "x_last")
        ww = [[None, None], [None, None]]
        ww[0][0] = weave_w(nc.scalar.copy, 0, 0)
        ww[1][0] = weave_w(nc.scalar.copy, 1, 0)
        shared = keep.tile([P, P, PACK], BF16, name="w_woven0_1", align_bytes=64)
        ww[0][1] = shared[:]
        weave(nc.scalar.copy, shared[:], w_sb[0][1][:])
        wq00 = quantize("w00", ww[0][0], P)
        half0 = psum.tile([P, HALF], F32, name="half0")
        late = psum.tile([P, U], F32, name="late")
        halves = [half0[:], late[:, 0:HALF]]
        for h in range(2):
            cols = slice(h * HALF, (h + 1) * HALF)
            multiply(halves[h], (xq0[0][:, cols], xq0[1][:, cols]), wq00)
        xq1 = quantize("x1", x_woven[1][:], V, "w_sb0_0")
        wq10 = quantize("w10", ww[1][0], P)
        for h in range(2):
            cols = slice(h * HALF, (h + 1) * HALF)
            multiply(first1[h][:], (xq1[0][:, cols], xq1[1][:, cols]), wq10)
        last = keep.tile([P, P, PACK], BF16, name="w_woven1_1", align_bytes=64)
        ww[1][1] = last[:]
        weave(nc.vector.tensor_copy, last[:, 0:SHARE, :], w_sb[1][1][:, :, 0:SHARE])
        wq01 = quantize("w01", ww[0][1], P)
        y00a = keep.tile([P, HEAD], F32, name="y00a", tag="w_woven1_0", align_bytes=64)
        nc.scalar.copy(y00a[:, 0:HALF], halves[0])
        nc.scalar.copy(y00a[:, HALF:HEAD], halves[1][:, 0:HEAD - HALF])
        weave(nc.scalar.copy, last[:, SHARE:P, :], w_sb[1][1][:, :, SHARE:P])
        early = psum.tile([P, HALF], F32, name="early")
        multiply(early[:], (xq0[0][:, HALF:V], xq0[1][:, HALF:V]), wq01)
        multiply(late[:, HALF:V], (xq0[0][:, 0:HALF], xq0[1][:, 0:HALF]), wq01)
        y10 = keep.tile([P, V], F32, name="y10", tag="w_sb0_1", align_bytes=64)
        for h in range(2):
            nc.vector.tensor_copy(y10[:, h * HALF:(h + 1) * HALF], first1[h][:])
        multiply(late[:, V:U], xq1, quantize("w11", ww[1][1], P, "w10"))
        nc.scalar.activation(cells[0][0][:].indirect(entries(to_sb[0], 0, HEAD)), y00a[:], COPY)
        scatter_v(1, 0, y10[:])
        rest = V - HEAD
        y0 = keep.tile([P, rest + V], F32, name="y0", align_bytes=64)
        nc.scalar.copy(y0[:, rest + HALF:rest + V], early[:])
        nc.scalar.copy(y0[:, 0:rest + HALF], late[:, HALF - rest:V])
        y11 = leave(nc.scalar.copy, "y11", late[:, V:U])
        nc.scalar.activation(cells[0][0][:].indirect(entries(to_sb[0], HEAD, V)), y0[:, 0:rest], COPY)
        scatter_s(0, 1, y0[:, rest:rest + V])
        scatter_v(1, 1, y11[:])
        total0 = keep.tile([P, V], F32, name="total0")
        nc.gpsimd.tensor_tensor(total0[:], cells[0][0][:, 0:V], cells[1][0][:, 0:V], ADD)
        nc.vector.tensor_tensor(cells[0][0][:, 0:V], cells[0][0][:, V:U], cells[1][0][:, V:U], ADD)
        store(0, 0, V, total0[:], relu_s, nc.scalar)
        store(0, V, U, cells[0][0][:, 0:V], relu_s, nc.scalar)
        totals = [cells[1][0][:, lo:hi] for lo, hi in CUTS]
        for h, (lo, hi) in enumerate(CUTS):
            nc.vector.tensor_tensor(totals[h], cells[0][1][:, lo:hi], cells[1][1][:, lo:hi], ADD)
        for h, relu in enumerate([relu_v, relu_v]):
            store(1, CUTS[h][0], CUTS[h][1], totals[h], relu, nc.sync)
